import numpy as np
import ml_dtypes


def mxq(x, axis, fmt="e4m3"):
    dtype, down = {"e4m3": (ml_dtypes.float8_e4m3fn, 7), "e5m2": (ml_dtypes.float8_e5m2, 14)}[fmt]
    v = np.moveaxis(np.asarray(x, np.float32).astype(ml_dtypes.bfloat16).astype(np.float64), axis, -1)
    blocks = v.reshape(v.shape[:-1] + (-1, 32))
    amax = np.abs(blocks).max(-1, keepdims=True)
    byte = np.maximum(np.where(amax > 0, np.frexp(amax)[1] - 1 + 127, 0) - down, 1)
    scale = np.exp2(byte - 127.0)
    codes = (blocks / scale).astype(np.float32).astype(dtype).astype(np.float64)
    return np.moveaxis((codes * scale).reshape(v.shape), -1, axis)


WIDE = False


def mx_kscale(k):
    if not WIDE:
        return np.ones(k)
    levels = np.array([10, -10, 5, -5, 0])
    if k % 512:
        return np.exp2(np.random.permutation(np.resize(levels, k // 32))).repeat(32)
    a = np.empty((k // 512, 16))
    for p in range(k // 512):
        a[p, :8] = np.random.permutation(np.resize(levels, 8))
        for g in range(8):
            far = levels[np.abs(levels - a[p, g]) >= 10]
            a[p, g + 8] = far[np.random.randint(len(far))]
    return np.exp2(a.ravel()).repeat(32)


def f64(x):
    return np.asarray(x).astype(np.float64)


def striped8(idx):
    return np.concatenate([x.reshape(-1, 16).T for x in idx]).astype(np.uint16)


def runs(offs, k):
    lists = np.stack([offs[16 * r : 16 * r + 16].T.reshape(-1) for r in range(8)]).astype(np.int64)
    return lists[np.arange(k) % 512 // 64]


def pack_weight(w):
    k, n = w.shape
    w = f64(np.asarray(w, np.float32).astype(ml_dtypes.bfloat16)).reshape(k // 32, 32, n)
    amax = np.abs(w).max(1)
    byte = np.clip(np.where(amax > 0, np.frexp(amax)[1] - 1 + 127 - 7, 1), 1, 254)
    scaled = (w * np.exp2(127.0 - byte)[:, None, :]).reshape(k, n).astype(np.float32)
    words = np.ascontiguousarray(scaled.reshape(k // 512, 128, 4, n).transpose(0, 1, 3, 2)).astype(ml_dtypes.float8_e4m3fn).view(np.uint8)
    return words, np.ascontiguousarray(byte.astype(np.uint8).reshape(k // 512, 16, n))


def unpack_weight(words, scales):
    g, p, n, _ = words.shape
    vals = np.ascontiguousarray(words).view(ml_dtypes.float8_e4m3fn).astype(np.float64) * np.repeat(np.exp2(scales.astype(np.float64) - 127.0), 8, axis=1)[..., None]
    return vals.transpose(0, 1, 3, 2).reshape(g * 512, n)


E2M1 = np.array([0.0, 0.5, 1.0, 1.5, 2.0, 3.0, 4.0, 6.0, -0.0, -0.5, -1.0, -1.5, -2.0, -3.0, -4.0, -6.0])


def pack_fp4(w):
    k, n = w.shape
    w = f64(np.asarray(w, np.float32).astype(ml_dtypes.bfloat16)).reshape(k // 32, 32, n)
    amax = np.abs(w).max(1)
    mant, ex = np.frexp(amax / 6.0)
    byte = np.clip(np.where(amax > 0, np.where(mant > 0.5, ex, ex - 1) + 127, 1), 1, 254)
    scaled = (w * np.exp2(127.0 - byte)[:, None, :]).reshape(k, n).astype(np.float32)
    c = np.ascontiguousarray(scaled.reshape(k // 512, 128, 4, n).transpose(0, 1, 3, 2)).astype(ml_dtypes.float4_e2m1fn).view(np.uint8) & 0xF
    words = (c[..., 0::2] | (c[..., 1::2] << 4)).reshape(k // 512, 128, 2 * n)
    return np.ascontiguousarray(words), np.ascontiguousarray(byte.astype(np.uint8).reshape(k // 512, 16, n))


def unpack_fp4(words, scales):
    g, _, n = scales.shape
    words = np.ascontiguousarray(words).reshape(g, 128, n, 2)
    nib = np.empty((g, 128, n, 4), np.uint8)
    nib[..., 0::2] = words & 0xF
    nib[..., 1::2] = words >> 4
    vals = E2M1[nib] * np.repeat(np.exp2(scales.astype(np.float64) - 127.0), 8, axis=1)[..., None]
    return vals.transpose(0, 1, 3, 2).reshape(g * 512, n)


def sigmoid(v):
    return 1.0 / (1.0 + np.exp(-np.maximum(v, -700.0)))


K, T, S, N, H, W = 512, 2048, 512, 512, 512, 256


def setup_inputs():
    n = np.random.standard_normal
    s = mx_kscale(K)[:, None]
    u = mx_kscale(H)
    packed_xT = pack_weight(n((K, T)) * s)
    packed_w1 = pack_fp4(n((K, H)) / np.sqrt(K) / s)
    packed_w2 = pack_fp4(n((H, N)) / np.sqrt(H) / u[:, None])
    perm = np.stack([np.random.permutation(S) for _ in range(8)])
    return {
        "x_words": packed_xT[0],
        "x_scales": packed_xT[1],
        "w1_words": packed_w1[0],
        "w1_scales": packed_w1[1],
        "sl": np.random.uniform(1.5, 3.0, (H, 1)).astype(np.float32),
        "th": (0.5 * n((H, 1))).astype(np.float32),
        "gn": (np.random.uniform(0.5, 1.5, (H, 1)) * u[:, None]).astype(np.float32),
        "w2_words": packed_w2[0],
        "w2_scales": packed_w2[1],
        "offs": striped8(np.random.randint(0, T, (8, S))),
        "n1": striped8(np.stack([np.random.permutation(S) for _ in range(8)])),
        "n2": striped8(np.stack([np.random.permutation(S) for _ in range(8)])),
        "n3": striped8(perm[:, :W]),
        "n4": striped8(perm[:, W:]),
        "n5": striped8(np.stack([np.random.permutation(S) for _ in range(8)])),
    }


def reference(x_words, x_scales, w1_words, w1_scales, sl, th, gn, w2_words, w2_scales, offs, n1, n2, n3, n4, n5):
    xq = unpack_weight(x_words, x_scales)[np.arange(K)[:, None], runs(offs, K)]
    y = unpack_fp4(w1_words, w1_scales).T @ xq
    sg = sigmoid(f64(sl) * (y[np.arange(H)[:, None], runs(n1, H)] - f64(th)))
    z = f64(gn) * (1.5 * (y * (sg - (sg[np.arange(H)[:, None], runs(n2, H)]))))
    h = unpack_fp4(w2_words, w2_scales).T @ mxq(z, 0, "e4m3")
    pa = h[np.arange(N)[:, None], runs(n3, N)]
    pb = h[np.arange(N)[:, None], runs(n4, N)]
    rb = pa - pb
    ra = pa + pb
    ds = np.zeros((N, S))
    ds[np.arange(N)[:, None], runs(n3, N)] = ra
    dt = ds.copy()
    dt[np.arange(N)[:, None], runs(n4, N)] = rb
    return np.maximum(dt, dt[np.arange(N)[:, None], runs(n5, N)])

@@ -1,0 +1,263 @@
+from contextlib import ExitStack
+
+import concourse.mybir as mybir
+
+K, T, S, N, H, W = 512, 2048, 512, 512, 512, 256
+FLOPS = 2 * K * H * S + 2 * H * N * S
+
+F32 = mybir.dt.float32
+BF16 = mybir.dt.bfloat16
+I32 = mybir.dt.int32
+U32 = mybir.dt.uint32
+U16 = mybir.dt.uint16
+U8 = mybir.dt.uint8
+FP8X4 = mybir.dt.float8_e4m3fn_x4
+FP4X4 = mybir.dt.float4_e2m1fn_x4
+ALU = mybir.AluOpType
+ACT = mybir.ActivationFunctionType
+
+P = 128
+PACK = 4
+HALF = S // 2
+STRIPE = 16
+
+
+def tile_picked_hashedbhaarh_none_p_kernel(
+    tc, x_words, x_scales, w1_words, w1_scales, sl, th, gn, w2_words, w2_scales, offs, n1, n2, n3, n4, n5, out
+):
+    nc = tc.nc
+
+    def cols(h):
+        return slice(h * HALF, (h + 1) * HALF)
+
+    def entries(lst, h):
+        return lst[:, h * HALF // STRIPE : (h + 1) * HALF // STRIPE]
+
+    with ExitStack() as ctx:
+        keep = ctx.enter_context(tc.tile_pool(name="keep", bufs=1))
+        psum = ctx.enter_context(tc.psum_pool(name="psum", bufs=1))
+
+        def load_list(src, name):
+            lst = keep.tile(list(src.shape), U16, name=name)
+            nc.sync.dma_start(lst[:], src)
+            return lst
+
+        xs_table = keep.tile([P, T], U8, name="xs_table")
+        nc.gpsimd.memset(xs_table[:].bitcast(I32), 0)
+        w1s_raw = keep.tile([P, H], U8, name="w1s_raw")
+        nc.vector.memset(w1s_raw[:].bitcast(I32), 0)
+        xq_scale = keep.tile([P, S], U8, name="xq_scale", align_bytes=64)
+        nc.vector.memset(xq_scale[:].bitcast(I32), 0)
+
+        offs_t = load_list(offs, "offs_t")
+        xw_table = keep.tile([P, T], I32, name="xw_table")
+        nc.scalar.dma_start(xw_table[:], x_words[0].rearrange("p n t -> p (n t)").bitcast(I32))
+        nc.sync.dma_start(xs_table[:].bitcast(I32)[0:P:8, :], x_scales[0].bitcast(I32))
+        for q in range(4):
+            nc.sync.dma_start(
+                w1s_raw[:].bitcast(I32)[32 * q : 32 * q + 4, :], w1_scales[0].bitcast(I32)[4 * q : 4 * q + 4, :]
+            )
+        n1_t = load_list(n1, "n1_t")
+        n2_t = load_list(n2, "n2_t")
+        n3_t = load_list(n3, "n3_t")
+        n4_t = load_list(n4, "n4_t")
+        n5_t = load_list(n5, "n5_t")
+
+        def load_rowwise(src, name):
+            v = keep.tile([P, PACK], F32, name=name)
+            nc.gpsimd.dma_start(v[:], src.rearrange("(p t) o -> p (t o)", t=PACK))
+            return v
+
+        w1w_raw = keep.tile([P, 2 * H], U8, name="w1w_raw")
+        nc.gpsimd.dma_start(w1w_raw[:].bitcast(I32), w1_words[0].bitcast(I32))
+        w2w_raw = keep.tile([P, 2 * N], U8, name="w2w_raw")
+        nc.gpsimd.dma_start(w2w_raw[:].bitcast(I32), w2_words[0].bitcast(I32))
+        sl_t = load_rowwise(sl, "sl_t")
+        th_t = load_rowwise(th, "th_t")
+        gn_t = load_rowwise(gn, "gn_t")
+
+        def deal_words(raw, name):
+            dealt = keep.tile([P, 2 * PACK * P], U8, name=name, align_bytes=64)
+            nc.scalar.copy(
+                dealt[:].bitcast(U16).rearrange("p (t m) -> p t m", t=PACK),
+                raw[:].bitcast(U16).rearrange("p (m t) -> p t m", t=PACK),
+            )
+            return dealt
+
+        def deal_scales(raw, name):
+            dealt = keep.tile([P, PACK * P], U8, name=name, align_bytes=64)
+            nc.vector.tensor_copy(
+                dealt[:].rearrange("p (t m) -> p t m", t=PACK), raw[:].rearrange("p (m t) -> p t m", t=PACK)
+            )
+            return dealt
+
+        w1w = deal_words(w1w_raw, "w1w")
+
+        xs_picked = keep.tile([P, S], U8, name="xs_picked")
+        nc.vector.tensor_copy(xs_picked[:], xs_table[:].indirect(offs_t[:]))
+        for r in range(4):
+            queue = nc.sync if r % 2 == 0 else nc.scalar
+            queue.dma_start(xq_scale[:].bitcast(I32)[r:P:32, :], xs_picked[:].bitcast(I32)[8 * r : P : 32, :])
+        xq = keep.tile([P, S], U32, name="xq", align_bytes=64)
+        nc.vector.tensor_copy(xq[:], xw_table[:].bitcast(U32).indirect(offs_t[:]))
+        w1s = deal_scales(w1s_raw, "w1s")
+        for q in range(4):
+            nc.sync.dma_start(
+                w1s_raw[:].bitcast(I32)[32 * q : 32 * q + 4, :], w2_scales[0].bitcast(I32)[4 * q : 4 * q + 4, :]
+            )
+        w2w = deal_words(w2w_raw, "w2w")
+
+        bias = keep.tile([P, PACK], F32, name="bias")
+        nc.vector.scalar_tensor_tensor(bias[:], sl_t[:], -1.0, th_t[:], ALU.mult, ALU.mult)
+        gain = keep.tile([P, PACK], F32, name="gain")
+        nc.vector.tensor_scalar(gain[:], gn_t[:], -1.5, None, ALU.mult)
+
+        y = []
+        for t in range(PACK):
+            y_bank = psum.tile([P, S], F32, name="y_bank%d" % t, tag="bank%d" % t)
+            nc.tensor.matmul_mx(
+                out=y_bank[:],
+                lhsT=w1w[:, 2 * P * t : 2 * P * (t + 1)].bitcast(FP4X4),
+                lhsT_scale=w1s[:, P * t : P * (t + 1)],
+                rhs=xq[:].bitcast(FP8X4),
+                rhs_scale=xq_scale[:],
+                start=True,
+                stop=True,
+            )
+            y_t = keep.tile([P, S], F32, name="y%d" % t)
+            nc.vector.tensor_copy(y_t[:], y_bank[:])
+            y.append(y_t)
+        w2s = deal_scales(w1s_raw, "w2s")
+
+        sg = []
+        for t in range(PACK):
+            sg_t = keep.tile([P, S], F32, name="sg%d" % t)
+            for h in range(2):
+                nc.scalar.activation(
+                    out=sg_t[:, cols(h)],
+                    in_=y[t][:].indirect(entries(n1_t, h)),
+                    func=ACT.Sigmoid,
+                    scale=sl_t[:, t : t + 1],
+                    bias=bias[:, t : t + 1],
+                )
+            sg.append(sg_t)
+
+        z_planes = keep.tile([P, 2, PACK, HALF], BF16, name="z_planes")
+        diff = [keep.tile([P, S], F32, name="diff%d" % t) for t in range(PACK)]
+        twin = [keep.tile([P, S], F32, name="twin%d" % t) for t in range(PACK)]
+
+        def fused_diff(t):
+            for h in range(2):
+                nc.vector.tensor_tensor(
+                    diff[t][:, cols(h)], sg[t][:].indirect(entries(n2_t, h)), twin[t][:, cols(h)], ALU.subtract
+                )
+
+        def z_whole(t):
+            nc.vector.scalar_tensor_tensor(
+                z_planes[:, :, t, :],
+                diff[t][:].rearrange("p (h c) -> p h c", h=2),
+                gain[:, t : t + 1],
+                y[t][:].rearrange("p (h c) -> p h c", h=2),
+                ALU.mult,
+                ALU.mult,
+            )
+
+        nc.vector.tensor_copy(twin[0][:], sg[0][:])
+        fused_diff(0)
+        nc.vector.tensor_copy(twin[1][:], sg[1][:])
+        z_whole(0)
+        fused_diff(1)
+        z_whole(1)
+
+        z_codes = keep.tile([P, S], U32, name="z_codes", align_bytes=64)
+        z_scale = keep.tile([P, S], U8, name="z_scale", align_bytes=64)
+        grouped = []
+        for h in range(2):
+            for t in (2, 3):
+                nc.scalar.activation(out=twin[t][:, cols(h)], in_=sg[t][:].indirect(entries(n2_t, h)), func=ACT.Copy)
+            for t in (2, 3):
+                nc.vector.tensor_tensor(diff[t][:, cols(h)], twin[t][:, cols(h)], sg[t][:, cols(h)], ALU.subtract)
+            for t in (2, 3):
+                nc.vector.scalar_tensor_tensor(
+                    z_planes[:, h, t, :], diff[t][:, cols(h)], gain[:, t : t + 1], y[t][:, cols(h)], ALU.mult, ALU.mult
+                )
+        for h in range(2):
+            g_h = keep.tile([P, HALF, PACK], BF16, name="grouped%d" % h, align_bytes=64)
+            dst = g_h[:].rearrange("p (c i) t -> p c t i", i=4)
+            src = z_planes[:, h, :, :].rearrange("p t (c i) -> p c t i", i=4)
+            if h == 0:
+                nc.scalar.copy(dst, src)
+            else:
+                nc.vector.tensor_copy(dst, src)
+            grouped.append(g_h)
+        for h in range(2):
+            nc.vector.quantize_mx(
+                out=z_codes[:, cols(h)].bitcast(FP8X4),
+                scales=z_scale[:, cols(h)],
+                in_=grouped[h][:].rearrange("p c t -> p (c t)"),
+            )
+
+        h_bank = {}
+        for t in range(PACK):
+            for h in range(2):
+                h_bank[t, h] = psum.tile([P, HALF], F32, name="h_bank%d_%d" % (t, h), tag="bank%d" % (PACK * (1 - h) + t))
+                nc.tensor.matmul_mx(
+                    out=h_bank[t, h][:],
+                    lhsT=w2w[:, 2 * P * t : 2 * P * (t + 1)].bitcast(FP4X4),
+                    lhsT_scale=w2s[:, P * t : P * (t + 1)],
+                    rhs=z_codes[:, cols(h)].bitcast(FP8X4),
+                    rhs_scale=z_scale[:, cols(h)],
+                    start=True,
+                    stop=True,
+                )
+
+        out_rows = out.rearrange("(p t) j -> t p j", t=PACK)
+        dt = [keep.tile([P, S], F32, name="dt%d" % t) for t in range(PACK)]
+        pa = [keep.tile([P, W], F32, name="pa%d" % t) for t in range(PACK)]
+        pb = [keep.tile([P, W], F32, name="pb%d" % t) for t in range(PACK)]
+        pb_neg = [keep.tile([P, W], F32, name="pb_neg%d" % t) for t in range(PACK)]
+        other = [keep.tile([P, S], F32, name="other%d" % t) for t in range(PACK)]
+        result = [keep.tile([P, S], F32, name="result%d" % t) for t in range(PACK)]
+
+        def fetch_pairs(t):
+            h_t = keep.tile([P, S], F32, name="h%d" % t)
+            nc.scalar.copy(h_t[:, cols(0)], h_bank[t, 0][:])
+            if t == 0:
+                nc.vector.tensor_copy(h_t[:, cols(1)], h_bank[t, 1][:])
+                nc.vector.tensor_copy(pa[t][:], h_t[:].indirect(n3_t[:]))
+            else:
+                nc.scalar.copy(h_t[:, cols(1)], h_bank[t, 1][:])
+                nc.scalar.activation(out=pa[t][:], in_=h_t[:].indirect(n3_t[:]), func=ACT.Copy)
+            nc.scalar.activation(out=pb[t][:], in_=h_t[:].indirect(n4_t[:]), func=ACT.Copy)
+
+        def negate(t):
+            nc.scalar.activation(out=pb_neg[t][:], in_=pb[t][:], func=ACT.Copy, scale=-1.0)
+
+        def fetch_other(t):
+            for h in range(2):
+                if t == PACK - 1 and h == 0:
+                    nc.vector.tensor_copy(other[t][:, cols(h)], dt[t][:].indirect(entries(n5_t, h)))
+                else:
+                    nc.scalar.activation(
+                        out=other[t][:, cols(h)], in_=dt[t][:].indirect(entries(n5_t, h)), func=ACT.Copy
+                    )
+
+        def finish(t, part):
+            nc.vector.tensor_tensor(result[t][:, part], dt[t][:, part], other[t][:, part], ALU.max)
+            nc.sync.dma_start(out_rows[t][:, part], result[t][:, part])
+
+        fetch_pairs(0)
+        negate(0)
+        fetch_pairs(1)
+        for t in range(PACK):
+            if t + 2 < PACK:
+                fetch_pairs(t + 2)
+            nc.vector.tensor_tensor(dt[t][:].indirect(n3_t[:]), pa[t][:], pb[t][:], ALU.add)
+            if t > 0:
+                finish(t - 1, slice(0, S))
+            nc.vector.tensor_tensor(dt[t][:].indirect(n4_t[:]), pa[t][:], pb_neg[t][:], ALU.add)
+            fetch_other(t)
+            if t + 1 < PACK:
+                negate(t + 1)
+        for h in range(2):
+            finish(PACK - 1, cols(h))

@@ -42,34 +42,34 @@ def tile_picked_hashedbhaarh_none_p_kernel(
             nc.sync.dma_start(lst[:], src)
             return lst
 
-        xs_table = keep.tile([P, T], U8, name="xs_table")
+        xs_table = keep.tile([P, T], U8, name="xs_table", tag="staged_scales")
         nc.gpsimd.memset(xs_table[:].bitcast(I32), 0)
         w1s_raw = keep.tile([P, H], U8, name="w1s_raw")
-        nc.vector.memset(w1s_raw[:].bitcast(I32), 0)
+        nc.gpsimd.memset(w1s_raw[:].bitcast(I32), 0)
         xq_scale = keep.tile([P, S], U8, name="xq_scale", align_bytes=64)
         nc.vector.memset(xq_scale[:].bitcast(I32), 0)
 
         offs_t = load_list(offs, "offs_t")
-        xw_table = keep.tile([P, T], I32, name="xw_table")
-        nc.scalar.dma_start(xw_table[:], x_words[0].rearrange("p n t -> p (n t)").bitcast(I32))
         nc.sync.dma_start(xs_table[:].bitcast(I32)[0:P:8, :], x_scales[0].bitcast(I32))
-        for q in range(4):
-            nc.sync.dma_start(
-                w1s_raw[:].bitcast(I32)[32 * q : 32 * q + 4, :], w1_scales[0].bitcast(I32)[4 * q : 4 * q + 4, :]
-            )
         n1_t = load_list(n1, "n1_t")
         n2_t = load_list(n2, "n2_t")
+        xw_table = keep.tile([P, T], I32, name="xw_table")
+        nc.sync.dma_start(xw_table[:], x_words[0].rearrange("p n t -> p (n t)").bitcast(I32))
+        w1w_raw = keep.tile([P, 2 * H], U8, name="w1w_raw")
+        nc.sync.dma_start(w1w_raw[:].bitcast(I32), w1_words[0].bitcast(I32))
         n3_t = load_list(n3, "n3_t")
         n4_t = load_list(n4, "n4_t")
         n5_t = load_list(n5, "n5_t")
+        for q in range(4):
+            nc.scalar.dma_start(
+                w1s_raw[:].bitcast(I32)[32 * q : 32 * q + 4, :], w1_scales[0].bitcast(I32)[4 * q : 4 * q + 4, :]
+            )
 
         def load_rowwise(src, name):
             v = keep.tile([P, PACK], F32, name=name)
             nc.gpsimd.dma_start(v[:], src.rearrange("(p t) o -> p (t o)", t=PACK))
             return v
 
-        w1w_raw = keep.tile([P, 2 * H], U8, name="w1w_raw")
-        nc.gpsimd.dma_start(w1w_raw[:].bitcast(I32), w1_words[0].bitcast(I32))
         w2w_raw = keep.tile([P, 2 * N], U8, name="w2w_raw")
         nc.gpsimd.dma_start(w2w_raw[:].bitcast(I32), w2_words[0].bitcast(I32))
         sl_t = load_rowwise(sl, "sl_t")
@@ -96,23 +96,29 @@ def tile_picked_hashedbhaarh_none_p_kernel(
         xs_picked = keep.tile([P, S], U8, name="xs_picked")
         nc.vector.tensor_copy(xs_picked[:], xs_table[:].indirect(offs_t[:]))
         for r in range(4):
-            queue = nc.sync if r % 2 == 0 else nc.scalar
+            queue = nc.scalar if r % 2 == 0 else nc.sync
             queue.dma_start(xq_scale[:].bitcast(I32)[r:P:32, :], xs_picked[:].bitcast(I32)[8 * r : P : 32, :])
+        w2s_raw = keep.tile([P, N], U8, name="w2s_raw", tag="staged_scales")
+        nc.vector.memset(w2s_raw[:].bitcast(I32), 0)
+        for q in range(4):
+            nc.sync.dma_start(
+                w2s_raw[:].bitcast(I32)[32 * q : 32 * q + 4, :], w2_scales[0].bitcast(I32)[4 * q : 4 * q + 4, :]
+            )
         xq = keep.tile([P, S], U32, name="xq", align_bytes=64)
         nc.vector.tensor_copy(xq[:], xw_table[:].bitcast(U32).indirect(offs_t[:]))
         w1s = deal_scales(w1s_raw, "w1s")
-        for q in range(4):
-            nc.sync.dma_start(
-                w1s_raw[:].bitcast(I32)[32 * q : 32 * q + 4, :], w2_scales[0].bitcast(I32)[4 * q : 4 * q + 4, :]
-            )
+        w2s = deal_scales(w2s_raw, "w2s")
         w2w = deal_words(w2w_raw, "w2w")
 
         bias = keep.tile([P, PACK], F32, name="bias")
-        nc.vector.scalar_tensor_tensor(bias[:], sl_t[:], -1.0, th_t[:], ALU.mult, ALU.mult)
+        sl_th = keep.tile([P, PACK], F32, name="sl_th")
+        nc.gpsimd.tensor_tensor(sl_th[:], sl_t[:], th_t[:], ALU.mult)
+        nc.gpsimd.tensor_scalar(bias[:], sl_th[:], -1.0, 0.0, ALU.mult, ALU.add)
         gain = keep.tile([P, PACK], F32, name="gain")
-        nc.vector.tensor_scalar(gain[:], gn_t[:], -1.5, None, ALU.mult)
+        nc.gpsimd.tensor_scalar(gain[:], gn_t[:], -1.5, 0.0, ALU.mult, ALU.add)
 
         y = []
+        y_gain = keep.tile([P, 2, PACK, HALF], F32, name="y_gain")
         for t in range(PACK):
             y_bank = psum.tile([P, S], F32, name="y_bank%d" % t, tag="bank%d" % t)
             nc.tensor.matmul_mx(
@@ -127,7 +133,9 @@ def tile_picked_hashedbhaarh_none_p_kernel(
             y_t = keep.tile([P, S], F32, name="y%d" % t)
             nc.vector.tensor_copy(y_t[:], y_bank[:])
             y.append(y_t)
-        w2s = deal_scales(w1s_raw, "w2s")
+            nc.gpsimd.tensor_scalar(
+                y_gain[:, :, t, :], y_t[:].rearrange("p (h c) -> p h c", h=2), gain[:, t : t + 1], 0.0, ALU.mult, ALU.add
+            )
 
         sg = []
         for t in range(PACK):
@@ -142,60 +150,57 @@ def tile_picked_hashedbhaarh_none_p_kernel(
                 )
             sg.append(sg_t)
 
-        z_planes = keep.tile([P, 2, PACK, HALF], BF16, name="z_planes")
-        diff = [keep.tile([P, S], F32, name="diff%d" % t) for t in range(PACK)]
+        diff = keep.tile([P, 2, PACK, HALF], F32, name="diff")
         twin = [keep.tile([P, S], F32, name="twin%d" % t) for t in range(PACK)]
 
-        def fused_diff(t):
-            for h in range(2):
-                nc.vector.tensor_tensor(
-                    diff[t][:, cols(h)], sg[t][:].indirect(entries(n2_t, h)), twin[t][:, cols(h)], ALU.subtract
-                )
-
-        def z_whole(t):
-            nc.vector.scalar_tensor_tensor(
-                z_planes[:, :, t, :],
-                diff[t][:].rearrange("p (h c) -> p h c", h=2),
-                gain[:, t : t + 1],
-                y[t][:].rearrange("p (h c) -> p h c", h=2),
-                ALU.mult,
-                ALU.mult,
+        def fused_diff(t, h):
+            nc.vector.tensor_tensor(
+                diff[:, h, t, :], sg[t][:].indirect(entries(n2_t, h)), twin[t][:, cols(h)], ALU.subtract
             )
 
-        nc.vector.tensor_copy(twin[0][:], sg[0][:])
-        fused_diff(0)
-        nc.vector.tensor_copy(twin[1][:], sg[1][:])
-        z_whole(0)
-        fused_diff(1)
-        z_whole(1)
+        def fetch_twin(t, h):
+            nc.scalar.activation(out=twin[t][:, cols(h)], in_=sg[t][:].indirect(entries(n2_t, h)), func=ACT.Copy)
+
+        def plain_diff(t, h):
+            nc.vector.tensor_tensor(diff[:, h, t, :], twin[t][:, cols(h)], sg[t][:, cols(h)], ALU.subtract)
 
         z_codes = keep.tile([P, S], U32, name="z_codes", align_bytes=64)
         z_scale = keep.tile([P, S], U8, name="z_scale", align_bytes=64)
-        grouped = []
-        for h in range(2):
-            for t in (2, 3):
-                nc.scalar.activation(out=twin[t][:, cols(h)], in_=sg[t][:].indirect(entries(n2_t, h)), func=ACT.Copy)
-            for t in (2, 3):
-                nc.vector.tensor_tensor(diff[t][:, cols(h)], twin[t][:, cols(h)], sg[t][:, cols(h)], ALU.subtract)
-            for t in (2, 3):
-                nc.vector.scalar_tensor_tensor(
-                    z_planes[:, h, t, :], diff[t][:, cols(h)], gain[:, t : t + 1], y[t][:, cols(h)], ALU.mult, ALU.mult
-                )
-        for h in range(2):
-            g_h = keep.tile([P, HALF, PACK], BF16, name="grouped%d" % h, align_bytes=64)
-            dst = g_h[:].rearrange("p (c i) t -> p c t i", i=4)
-            src = z_planes[:, h, :, :].rearrange("p t (c i) -> p c t i", i=4)
-            if h == 0:
-                nc.scalar.copy(dst, src)
-            else:
-                nc.vector.tensor_copy(dst, src)
-            grouped.append(g_h)
-        for h in range(2):
+        grouped = [keep.tile([P, HALF, PACK], BF16, name="grouped%d" % h, align_bytes=64) for h in range(2)]
+
+        def z_half(h):
+            nc.vector.tensor_tensor(
+                grouped[h][:].rearrange("p (c i) t -> p c t i", i=4),
+                diff[:, h, :, :].rearrange("p t (c i) -> p c t i", i=4),
+                y_gain[:, h, :, :].rearrange("p t (c i) -> p c t i", i=4),
+                ALU.mult,
+            )
+
+        def quantise(h):
             nc.vector.quantize_mx(
                 out=z_codes[:, cols(h)].bitcast(FP8X4),
                 scales=z_scale[:, cols(h)],
                 in_=grouped[h][:].rearrange("p c t -> p (c t)"),
             )
+
+        nc.vector.tensor_copy(twin[0][:], sg[0][:])
+        fused_diff(0, 0)
+        fused_diff(0, 1)
+        nc.vector.tensor_copy(twin[1][:], sg[1][:])
+        nc.vector.tensor_copy(twin[2][:, cols(0)], sg[2][:, cols(0)])
+        fused_diff(1, 0)
+        fused_diff(1, 1)
+        fused_diff(2, 0)
+        fetch_twin(3, 0)
+        fetch_twin(2, 1)
+        fetch_twin(3, 1)
+        plain_diff(3, 0)
+        plain_diff(2, 1)
+        z_half(0)
+        plain_diff(3, 1)
+        quantise(0)
+        z_half(1)
+        quantise(1)
 
         h_bank = {}
         for t in range(PACK):

@@ -49,6 +49,11 @@ def tile_picked_hashedbhaarh_none_p_kernel(
         xq_scale = keep.tile([P, S], U8, name="xq_scale", align_bytes=64)
         nc.vector.memset(xq_scale[:].bitcast(I32), 0)
 
+        warm_in = keep.tile([P, 1], F32, name="warm_in")
+        nc.vector.memset(warm_in[:], 0.0)
+        warm_out = keep.tile([P, 1], F32, name="warm_out")
+        nc.scalar.activation(out=warm_out[:], in_=warm_in[:], func=ACT.Sigmoid)
+
         offs_t = load_list(offs, "offs_t")
         nc.sync.dma_start(xs_table[:].bitcast(I32)[0:P:8, :], x_scales[0].bitcast(I32))
         n1_t = load_list(n1, "n1_t")

@@ -123,24 +123,44 @@ def tile_picked_hashedbhaarh_none_p_kernel(
         nc.gpsimd.tensor_scalar(gain[:], gn_t[:], -1.5, 0.0, ALU.mult, ALU.add)
 
         y = []
+        y_banks = []
         y_gain = keep.tile([P, 2, PACK, HALF], F32, name="y_gain")
-        for t in range(PACK):
-            y_bank = psum.tile([P, S], F32, name="y_bank%d" % t, tag="bank%d" % t)
+
+        def first_product(bank, t, part):
             nc.tensor.matmul_mx(
-                out=y_bank[:],
+                out=bank[:],
                 lhsT=w1w[:, 2 * P * t : 2 * P * (t + 1)].bitcast(FP4X4),
                 lhsT_scale=w1s[:, P * t : P * (t + 1)],
-                rhs=xq[:].bitcast(FP8X4),
-                rhs_scale=xq_scale[:],
+                rhs=xq[:, part].bitcast(FP8X4),
+                rhs_scale=xq_scale[:, part],
                 start=True,
                 stop=True,
             )
+
+        for t in range(PACK):
             y_t = keep.tile([P, S], F32, name="y%d" % t)
-            nc.vector.tensor_copy(y_t[:], y_bank[:])
+            if t == 0:
+                y_bank = psum.tile([P, HALF], F32, name="y_bank0_low", tag="bank0")
+                y_bank_high = psum.tile([P, HALF], F32, name="y_bank0_high", tag="bank%d" % PACK)
+                first_product(y_bank, t, cols(0))
+                first_product(y_bank_high, t, cols(1))
+                nc.vector.tensor_copy(y_t[:, cols(0)], y_bank[:])
+                nc.scalar.copy(y_t[:, cols(1)], y_bank_high[:])
+            else:
+                y_bank = psum.tile([P, S], F32, name="y_bank%d" % t, tag="bank%d" % t)
+                first_product(y_bank, t, slice(0, S))
+                nc.vector.tensor_copy(y_t[:], y_bank[:])
             y.append(y_t)
-            nc.gpsimd.tensor_scalar(
-                y_gain[:, :, t, :], y_t[:].rearrange("p (h c) -> p h c", h=2), gain[:, t : t + 1], 0.0, ALU.mult, ALU.add
-            )
+            y_banks.append(y_bank)
+            if t < PACK - 1:
+                nc.gpsimd.tensor_scalar(
+                    y_gain[:, :, t, :],
+                    y_t[:].rearrange("p (h c) -> p h c", h=2),
+                    gain[:, t : t + 1],
+                    0.0,
+                    ALU.mult,
+                    ALU.add,
+                )
 
         sg = []
         for t in range(PACK):
@@ -165,6 +185,12 @@ def tile_picked_hashedbhaarh_none_p_kernel(
 
         def fetch_twin(t, h):
             nc.scalar.activation(out=twin[t][:, cols(h)], in_=sg[t][:].indirect(entries(n2_t, h)), func=ACT.Copy)
+
+        def last_gain(h):
+            t = PACK - 1
+            nc.scalar.activation(
+                out=y_gain[:, h, t, :], in_=y_banks[t][:, cols(h)], func=ACT.Copy, scale=gain[:, t : t + 1]
+            )
 
         def plain_diff(t, h):
             nc.vector.tensor_tensor(diff[:, h, t, :], twin[t][:, cols(h)], sg[t][:, cols(h)], ALU.subtract)
@@ -196,8 +222,10 @@ def tile_picked_hashedbhaarh_none_p_kernel(
         fused_diff(1, 0)
         fused_diff(1, 1)
         fused_diff(2, 0)
+        last_gain(0)
         fetch_twin(3, 0)
         fetch_twin(2, 1)
+        last_gain(1)
         fetch_twin(3, 1)
         plain_diff(3, 0)
         plain_diff(2, 1)
@@ -252,9 +280,9 @@ def tile_picked_hashedbhaarh_none_p_kernel(
                         out=other[t][:, cols(h)], in_=dt[t][:].indirect(entries(n5_t, h)), func=ACT.Copy
                     )
 
-        def finish(t, part):
+        def finish(t, part, queue):
             nc.vector.tensor_tensor(result[t][:, part], dt[t][:, part], other[t][:, part], ALU.max)
-            nc.sync.dma_start(out_rows[t][:, part], result[t][:, part])
+            queue.dma_start(out_rows[t][:, part], result[t][:, part])
 
         fetch_pairs(0)
         negate(0)
@@ -264,10 +292,10 @@ def tile_picked_hashedbhaarh_none_p_kernel(
                 fetch_pairs(t + 2)
             nc.vector.tensor_tensor(dt[t][:].indirect(n3_t[:]), pa[t][:], pb[t][:], ALU.add)
             if t > 0:
-                finish(t - 1, slice(0, S))
+                finish(t - 1, slice(0, S), nc.sync)
             nc.vector.tensor_tensor(dt[t][:].indirect(n4_t[:]), pa[t][:], pb_neg[t][:], ALU.add)
             fetch_other(t)
             if t + 1 < PACK:
                 negate(t + 1)
         for h in range(2):
-            finish(PACK - 1, cols(h))
+            finish(PACK - 1, cols(h), nc.sync if h == 0 else nc.scalar)

from contextlib import ExitStack

import concourse.mybir as mybir

K, T, S, N, H, W = 512, 2048, 512, 512, 512, 256
FLOPS = 2 * K * H * S + 2 * H * N * S

F32 = mybir.dt.float32
BF16 = mybir.dt.bfloat16
I32 = mybir.dt.int32
U32 = mybir.dt.uint32
U16 = mybir.dt.uint16
U8 = mybir.dt.uint8
FP8X4 = mybir.dt.float8_e4m3fn_x4
FP4X4 = mybir.dt.float4_e2m1fn_x4
ALU = mybir.AluOpType
ACT = mybir.ActivationFunctionType

P = 128
PACK = 4
HALF = S // 2
STRIPE = 16


def tile_picked_hashedbhaarh_none_p_kernel(
    tc, x_words, x_scales, w1_words, w1_scales, sl, th, gn, w2_words, w2_scales, offs, n1, n2, n3, n4, n5, out
):
    nc = tc.nc

    def cols(h):
        return slice(h * HALF, (h + 1) * HALF)

    def entries(lst, h):
        return lst[:, h * HALF // STRIPE : (h + 1) * HALF // STRIPE]

    with ExitStack() as ctx:
        keep = ctx.enter_context(tc.tile_pool(name="keep", bufs=1))
        psum = ctx.enter_context(tc.psum_pool(name="psum", bufs=1))

        def load_list(src, name):
            lst = keep.tile(list(src.shape), U16, name=name)
            nc.sync.dma_start(lst[:], src)
            return lst

        xs_table = keep.tile([P, T], U8, name="xs_table", tag="staged_scales")
        nc.gpsimd.memset(xs_table[:].bitcast(I32), 0)
        w1s_raw = keep.tile([P, H], U8, name="w1s_raw")
        nc.gpsimd.memset(w1s_raw[:].bitcast(I32), 0)
        xq_scale = keep.tile([P, S], U8, name="xq_scale", align_bytes=64)
        nc.vector.memset(xq_scale[:].bitcast(I32), 0)

        warm_in = keep.tile([P, 1], F32, name="warm_in")
        nc.vector.memset(warm_in[:], 0.0)
        warm_out = keep.tile([P, 1], F32, name="warm_out")
        nc.scalar.activation(out=warm_out[:], in_=warm_in[:], func=ACT.Sigmoid)

        offs_t = load_list(offs, "offs_t")
        nc.sync.dma_start(xs_table[:].bitcast(I32)[0:P:8, :], x_scales[0].bitcast(I32))
        n1_t = load_list(n1, "n1_t")
        n2_t = load_list(n2, "n2_t")
        xw_table = keep.tile([P, T], I32, name="xw_table")
        nc.sync.dma_start(xw_table[:], x_words[0].rearrange("p n t -> p (n t)").bitcast(I32))
        w1w_raw = keep.tile([P, 2 * H], U8, name="w1w_raw")
        nc.sync.dma_start(w1w_raw[:].bitcast(I32), w1_words[0].bitcast(I32))
        n3_t = load_list(n3, "n3_t")
        n4_t = load_list(n4, "n4_t")
        n5_t = load_list(n5, "n5_t")
        for q in range(4):
            nc.scalar.dma_start(
                w1s_raw[:].bitcast(I32)[32 * q : 32 * q + 4, :], w1_scales[0].bitcast(I32)[4 * q : 4 * q + 4, :]
            )

        def load_rowwise(src, name):
            v = keep.tile([P, PACK], F32, name=name)
            nc.gpsimd.dma_start(v[:], src.rearrange("(p t) o -> p (t o)", t=PACK))
            return v

        w2w_raw = keep.tile([P, 2 * N], U8, name="w2w_raw")
        nc.gpsimd.dma_start(w2w_raw[:].bitcast(I32), w2_words[0].bitcast(I32))
        sl_t = load_rowwise(sl, "sl_t")
        th_t = load_rowwise(th, "th_t")
        gn_t = load_rowwise(gn, "gn_t")

        def deal_words(raw, name):
            dealt = keep.tile([P, 2 * PACK * P], U8, name=name, align_bytes=64)
            nc.scalar.copy(
                dealt[:].bitcast(U16).rearrange("p (t m) -> p t m", t=PACK),
                raw[:].bitcast(U16).rearrange("p (m t) -> p t m", t=PACK),
            )
            return dealt

        def deal_scales(raw, name):
            dealt = keep.tile([P, PACK * P], U8, name=name, align_bytes=64)
            nc.vector.tensor_copy(
                dealt[:].rearrange("p (t m) -> p t m", t=PACK), raw[:].rearrange("p (m t) -> p t m", t=PACK)
            )
            return dealt

        w1w = deal_words(w1w_raw, "w1w")

        xs_picked = keep.tile([P, S], U8, name="xs_picked")
        nc.vector.tensor_copy(xs_picked[:], xs_table[:].indirect(offs_t[:]))
        for r in range(4):
            queue = nc.scalar if r % 2 == 0 else nc.sync
            queue.dma_start(xq_scale[:].bitcast(I32)[r:P:32, :], xs_picked[:].bitcast(I32)[8 * r : P : 32, :])
        w2s_raw = keep.tile([P, N], U8, name="w2s_raw", tag="staged_scales")
        nc.vector.memset(w2s_raw[:].bitcast(I32), 0)
        for q in range(4):
            nc.sync.dma_start(
                w2s_raw[:].bitcast(I32)[32 * q : 32 * q + 4, :], w2_scales[0].bitcast(I32)[4 * q : 4 * q + 4, :]
            )
        xq = keep.tile([P, S], U32, name="xq", align_bytes=64)
        nc.vector.tensor_copy(xq[:], xw_table[:].bitcast(U32).indirect(offs_t[:]))
        w1s = deal_scales(w1s_raw, "w1s")
        w2s = deal_scales(w2s_raw, "w2s")
        w2w = deal_words(w2w_raw, "w2w")

        bias = keep.tile([P, PACK], F32, name="bias")
        sl_th = keep.tile([P, PACK], F32, name="sl_th")
        nc.gpsimd.tensor_tensor(sl_th[:], sl_t[:], th_t[:], ALU.mult)
        nc.gpsimd.tensor_scalar(bias[:], sl_th[:], -1.0, 0.0, ALU.mult, ALU.add)
        gain = keep.tile([P, PACK], F32, name="gain")
        nc.gpsimd.tensor_scalar(gain[:], gn_t[:], -1.5, 0.0, ALU.mult, ALU.add)

        y = []
        y_banks = []
        y_gain = keep.tile([P, 2, PACK, HALF], F32, name="y_gain")

        def first_product(bank, t, part):
            nc.tensor.matmul_mx(
                out=bank[:],
                lhsT=w1w[:, 2 * P * t : 2 * P * (t + 1)].bitcast(FP4X4),
                lhsT_scale=w1s[:, P * t : P * (t + 1)],
                rhs=xq[:, part].bitcast(FP8X4),
                rhs_scale=xq_scale[:, part],
                start=True,
                stop=True,
            )

        for t in range(PACK):
            y_t = keep.tile([P, S], F32, name="y%d" % t)
            if t == 0:
                y_bank = psum.tile([P, HALF], F32, name="y_bank0_low", tag="bank0")
                y_bank_high = psum.tile([P, HALF], F32, name="y_bank0_high", tag="bank%d" % PACK)
                first_product(y_bank, t, cols(0))
                first_product(y_bank_high, t, cols(1))
                nc.vector.tensor_copy(y_t[:, cols(0)], y_bank[:])
                nc.scalar.copy(y_t[:, cols(1)], y_bank_high[:])
            else:
                y_bank = psum.tile([P, S], F32, name="y_bank%d" % t, tag="bank%d" % t)
                first_product(y_bank, t, slice(0, S))
                nc.vector.tensor_copy(y_t[:], y_bank[:])
            y.append(y_t)
            y_banks.append(y_bank)
            if t < PACK - 1:
                nc.gpsimd.tensor_scalar(
                    y_gain[:, :, t, :],
                    y_t[:].rearrange("p (h c) -> p h c", h=2),
                    gain[:, t : t + 1],
                    0.0,
                    ALU.mult,
                    ALU.add,
                )

        sg = []
        for t in range(PACK):
            sg_t = keep.tile([P, S], F32, name="sg%d" % t)
            for h in range(2):
                nc.scalar.activation(
                    out=sg_t[:, cols(h)],
                    in_=y[t][:].indirect(entries(n1_t, h)),
                    func=ACT.Sigmoid,
                    scale=sl_t[:, t : t + 1],
                    bias=bias[:, t : t + 1],
                )
            sg.append(sg_t)

        diff = keep.tile([P, 2, PACK, HALF], F32, name="diff")
        twin = [keep.tile([P, S], F32, name="twin%d" % t) for t in range(PACK)]

        def fused_diff(t, h):
            nc.vector.tensor_tensor(
                diff[:, h, t, :], sg[t][:].indirect(entries(n2_t, h)), twin[t][:, cols(h)], ALU.subtract
            )

        def fetch_twin(t, h):
            nc.scalar.activation(out=twin[t][:, cols(h)], in_=sg[t][:].indirect(entries(n2_t, h)), func=ACT.Copy)

        def last_gain(h):
            t = PACK - 1
            nc.scalar.activation(
                out=y_gain[:, h, t, :], in_=y_banks[t][:, cols(h)], func=ACT.Copy, scale=gain[:, t : t + 1]
            )

        def plain_diff(t, h):
            nc.vector.tensor_tensor(diff[:, h, t, :], twin[t][:, cols(h)], sg[t][:, cols(h)], ALU.subtract)

        z_codes = keep.tile([P, S], U32, name="z_codes", align_bytes=64)
        z_scale = keep.tile([P, S], U8, name="z_scale", align_bytes=64)
        grouped = [keep.tile([P, HALF, PACK], BF16, name="grouped%d" % h, align_bytes=64) for h in range(2)]

        def z_half(h):
            nc.vector.tensor_tensor(
                grouped[h][:].rearrange("p (c i) t -> p c t i", i=4),
                diff[:, h, :, :].rearrange("p t (c i) -> p c t i", i=4),
                y_gain[:, h, :, :].rearrange("p t (c i) -> p c t i", i=4),
                ALU.mult,
            )

        def quantise(h):
            nc.vector.quantize_mx(
                out=z_codes[:, cols(h)].bitcast(FP8X4),
                scales=z_scale[:, cols(h)],
                in_=grouped[h][:].rearrange("p c t -> p (c t)"),
            )

        nc.vector.tensor_copy(twin[0][:], sg[0][:])
        fused_diff(0, 0)
        fused_diff(0, 1)
        nc.vector.tensor_copy(twin[1][:], sg[1][:])
        nc.vector.tensor_copy(twin[2][:, cols(0)], sg[2][:, cols(0)])
        fused_diff(1, 0)
        fused_diff(1, 1)
        fused_diff(2, 0)
        last_gain(0)
        fetch_twin(3, 0)
        fetch_twin(2, 1)
        last_gain(1)
        fetch_twin(3, 1)
        plain_diff(3, 0)
        plain_diff(2, 1)
        z_half(0)
        plain_diff(3, 1)
        quantise(0)
        z_half(1)
        quantise(1)

        h_bank = {}
        for t in range(PACK):
            for h in range(2):
                h_bank[t, h] = psum.tile([P, HALF], F32, name="h_bank%d_%d" % (t, h), tag="bank%d" % (PACK * (1 - h) + t))
                nc.tensor.matmul_mx(
                    out=h_bank[t, h][:],
                    lhsT=w2w[:, 2 * P * t : 2 * P * (t + 1)].bitcast(FP4X4),
                    lhsT_scale=w2s[:, P * t : P * (t + 1)],
                    rhs=z_codes[:, cols(h)].bitcast(FP8X4),
                    rhs_scale=z_scale[:, cols(h)],
                    start=True,
                    stop=True,
                )

        out_rows = out.rearrange("(p t) j -> t p j", t=PACK)
        dt = [keep.tile([P, S], F32, name="dt%d" % t) for t in range(PACK)]
        pa = [keep.tile([P, W], F32, name="pa%d" % t) for t in range(PACK)]
        pb = [keep.tile([P, W], F32, name="pb%d" % t) for t in range(PACK)]
        pb_neg = [keep.tile([P, W], F32, name="pb_neg%d" % t) for t in range(PACK)]
        other = [keep.tile([P, S], F32, name="other%d" % t) for t in range(PACK)]
        result = [keep.tile([P, S], F32, name="result%d" % t) for t in range(PACK)]

        def fetch_pairs(t):
            h_t = keep.tile([P, S], F32, name="h%d" % t)
            nc.scalar.copy(h_t[:, cols(0)], h_bank[t, 0][:])
            if t == 0:
                nc.vector.tensor_copy(h_t[:, cols(1)], h_bank[t, 1][:])
                nc.vector.tensor_copy(pa[t][:], h_t[:].indirect(n3_t[:]))
            else:
                nc.scalar.copy(h_t[:, cols(1)], h_bank[t, 1][:])
                nc.scalar.activation(out=pa[t][:], in_=h_t[:].indirect(n3_t[:]), func=ACT.Copy)
            nc.scalar.activation(out=pb[t][:], in_=h_t[:].indirect(n4_t[:]), func=ACT.Copy)

        def negate(t):
            nc.scalar.activation(out=pb_neg[t][:], in_=pb[t][:], func=ACT.Copy, scale=-1.0)

        def fetch_other(t):
            for h in range(2):
                if t == PACK - 1 and h == 0:
                    nc.vector.tensor_copy(other[t][:, cols(h)], dt[t][:].indirect(entries(n5_t, h)))
                else:
                    nc.scalar.activation(
                        out=other[t][:, cols(h)], in_=dt[t][:].indirect(entries(n5_t, h)), func=ACT.Copy
                    )

        def finish(t, part, queue):
            nc.vector.tensor_tensor(result[t][:, part], dt[t][:, part], other[t][:, part], ALU.max)
            queue.dma_start(out_rows[t][:, part], result[t][:, part])

        fetch_pairs(0)
        negate(0)
        fetch_pairs(1)
        for t in range(PACK):
            if t + 2 < PACK:
                fetch_pairs(t + 2)
            nc.vector.tensor_tensor(dt[t][:].indirect(n3_t[:]), pa[t][:], pb[t][:], ALU.add)
            if t > 0:
                finish(t - 1, slice(0, S), nc.sync)
            nc.vector.tensor_tensor(dt[t][:].indirect(n4_t[:]), pa[t][:], pb_neg[t][:], ALU.add)
            fetch_other(t)
            if t + 1 < PACK:
                negate(t + 1)
        for h in range(2):
            finish(PACK - 1, cols(h), nc.sync if h == 0 else nc.scalar)
